import numpy as np
import ml_dtypes


def mxq(x, axis, fmt="e4m3"):
    dtype, down = {"e4m3": (ml_dtypes.float8_e4m3fn, 7), "e5m2": (ml_dtypes.float8_e5m2, 14)}[fmt]
    v = np.moveaxis(np.asarray(x, np.float32).astype(ml_dtypes.bfloat16).astype(np.float64), axis, -1)
    blocks = v.reshape(v.shape[:-1] + (-1, 32))
    amax = np.abs(blocks).max(-1, keepdims=True)
    byte = np.maximum(np.where(amax > 0, np.frexp(amax)[1] - 1 + 127, 0) - down, 1)
    scale = np.exp2(byte - 127.0)
    codes = (blocks / scale).astype(np.float32).astype(dtype).astype(np.float64)
    return np.moveaxis((codes * scale).reshape(v.shape), -1, axis)


WIDE = False


def mx_kscale(k):
    if not WIDE:
        return np.ones(k)
    levels = np.array([10, -10, 5, -5, 0])
    if k % 512:
        return np.exp2(np.random.permutation(np.resize(levels, k // 32))).repeat(32)
    a = np.empty((k // 512, 16))
    for p in range(k // 512):
        a[p, :8] = np.random.permutation(np.resize(levels, 8))
        for g in range(8):
            far = levels[np.abs(levels - a[p, g]) >= 10]
            a[p, g + 8] = far[np.random.randint(len(far))]
    return np.exp2(a.ravel()).repeat(32)


def f64(x):
    return np.asarray(x).astype(np.float64)


def striped(idx):
    return np.tile(idx.reshape(-1, 16).T, (8, 1)).astype(np.uint16)


def unstriped(offs):
    return offs[:16].T.reshape(-1).astype(np.int64)


def pack_weight(w):
    k, n = w.shape
    w = f64(np.asarray(w, np.float32).astype(ml_dtypes.bfloat16)).reshape(k // 32, 32, n)
    amax = np.abs(w).max(1)
    byte = np.clip(np.where(amax > 0, np.frexp(amax)[1] - 1 + 127 - 7, 1), 1, 254)
    scaled = (w * np.exp2(127.0 - byte)[:, None, :]).reshape(k, n).astype(np.float32)
    words = np.ascontiguousarray(scaled.reshape(k // 512, 128, 4, n).transpose(0, 1, 3, 2)).astype(ml_dtypes.float8_e4m3fn).view(np.uint8)
    return words, np.ascontiguousarray(byte.astype(np.uint8).reshape(k // 512, 16, n))


def unpack_weight(words, scales):
    g, p, n, _ = words.shape
    vals = np.ascontiguousarray(words).view(ml_dtypes.float8_e4m3fn).astype(np.float64) * np.repeat(np.exp2(scales.astype(np.float64) - 127.0), 8, axis=1)[..., None]
    return vals.transpose(0, 1, 3, 2).reshape(g * 512, n)

def planes(y):
    n, m = y.shape
    v = y.astype(np.float32).astype(ml_dtypes.bfloat16).astype(np.float64).reshape(n // 32, 32, m)
    top = np.abs(v).max(1)
    byte = np.clip(np.where(top > 0, np.frexp(top)[1] - 1 + 127 - 7, 1), 1, 254)
    codes = (v * np.exp2(127.0 - byte)[:, None, :]).reshape(n, m).astype(np.float32).astype(ml_dtypes.float8_e4m3fn).view(np.uint8)
    words = codes.reshape(n // 512, 128, 4, m).transpose(0, 1, 3, 2)
    return np.ascontiguousarray(words), np.ascontiguousarray(byte.astype(np.uint8).reshape(n // 512, 16, m))


K, T, S, H, W = 512, 2048, 512, 512, 384


def setup_inputs():
    n = np.random.standard_normal
    s = mx_kscale(K)[:, None]
    u = mx_kscale(S)
    packed_xT = pack_weight(n((K, T)) * s)
    return {
        "x_words": packed_xT[0],
        "x_scales": packed_xT[1],
        "wa": (n((K, H)) / np.sqrt(K) / s).astype(np.float32),
        "wb": (n((K, H)) / np.sqrt(K) / s).astype(np.float32),
        "gt": (np.random.uniform(0.5, 1.5, (S, 1)) * u[:, None]).astype(np.float32),
        "gi": (np.random.uniform(0.5, 1.5, (S, 1)) / u[:, None]).astype(np.float32),
        "offs": striped(np.random.permutation(T)[:S]),
        "two": striped(np.random.permutation(T)[:S]),
        "n1": striped(np.random.permutation(H)),
        "n2": striped(np.random.permutation(H)),
        "n3": striped(np.random.permutation(H)[:W]),
        "n4": striped(np.random.permutation(H)[:W]),
    }


def reference(x_words, x_scales, wa, wb, gt, gi, offs, two, n1, n2, n3, n4):
    xq = unpack_weight(x_words, x_scales)[:, unstriped(offs)]
    a = xq.T @ mxq(f64(wa), 0, "e4m3")
    x_two = unpack_weight(x_words, x_scales)[:, unstriped(two)]
    b = x_two.T @ mxq(f64(wb), 0, "e4m3")
    z = f64(gt) * (a * (np.tanh(b[:, unstriped(n1)] - b[:, unstriped(n2)])))
    z2 = f64(gi) * b
    cv = 0.0625 * ((mxq(z, 0, "e4m3").T @ mxq(z2, 0, "e4m3")))
    old = cv[:, unstriped(n3)]
    pa = cv[:, unstriped(n4)]
    ra = old - np.tanh(pa)
    out = cv.copy()
    out[:, unstriped(n3)] = ra
    return (out,) + planes(out)

@@ -1,0 +1,283 @@
+from contextlib import ExitStack
+
+import concourse.mybir as mybir
+
+K, T, S, H, W = 512, 2048, 512, 512, 384
+FLOPS = 3 * 2 * 512 * 512 * 512
+
+F32 = mybir.dt.float32
+BF16 = mybir.dt.bfloat16
+I32 = mybir.dt.int32
+U32 = mybir.dt.uint32
+U16 = mybir.dt.uint16
+U8 = mybir.dt.uint8
+FP8X4 = mybir.dt.float8_e4m3fn_x4
+ACT = mybir.ActivationFunctionType
+ALU = mybir.AluOpType
+
+P = 128
+PACK = 4
+PAD = 8
+HALF = 256
+EVAC_V = ()
+N2_S = (3,)
+Z2_S = ()
+FIRST = 2
+
+
+def tile_picked_momtjointbktanh_none_po_kernel(
+    tc, x_words, x_scales, wa, wb, gt, gi, offs, two, n1, n2, n3, n4, out_0, out_1, out_2
+):
+    nc = tc.nc
+    with ExitStack() as ctx:
+        keep = ctx.enter_context(tc.tile_pool(name="keep", bufs=1))
+        psum = ctx.enter_context(tc.psum_pool(name="psum", bufs=1))
+
+        def sb(name, shape, dtype, tag=None, bufs=1):
+            return keep.tile(shape, dtype, name=name, tag=tag or name, bufs=bufs, align_bytes=64)
+
+        def load_list(name, src):
+            t = keep.tile(list(src.shape), U16, name=name)
+            nc.sync.dma_start(t[:], src)
+            return t
+
+        wb_rows = wb.rearrange("(p j) n -> p j n", j=PACK)
+        wa_rows = wa.rearrange("(p j) n -> p j n", j=PACK)
+
+        def load_half(name, rows, h):
+            raw = sb(name, [P, PACK, HALF], F32)
+            nc.sync.dma_start(out=raw[:], in_=rows[:, :, h * HALF : (h + 1) * HALF])
+            return raw
+
+        xs = sb("xs", [P, T], U8)
+        nc.gpsimd.memset(xs[:].bitcast(I32), 0)
+        for q in range(4):
+            nc.scalar.dma_start(out=xs[32 * q : 32 * q + 4, :].bitcast(I32), in_=x_scales[0, 4 * q : 4 * q + 4, :].bitcast(I32))
+        two_t = load_list("two_t", two)
+        offs_t = load_list("offs_t", offs)
+        n1_t = load_list("n1_t", n1)
+        xw = sb("xw", [P, T], I32)
+        nc.sync.dma_start(out=xw[:], in_=x_words[0].rearrange("p c r -> p (c r)").bitcast(I32))
+        n2_t = load_list("n2_t", n2)
+        n3_t = load_list("n3_t", n3)
+        wb_raw = [load_half("wb_raw%d" % h, wb_rows, h) for h in range(2)]
+        wa_raw = [load_half("wa_raw%d" % h, wa_rows, h) for h in range(2)]
+        gi_t = sb("gi_t", [P, PACK], F32)
+        nc.sync.dma_start(out=gi_t[:], in_=gi.rearrange("(p t) o -> p (t o)", t=PACK))
+        gt_t = sb("gt_t", [P, PACK], F32)
+        nc.sync.dma_start(out=gt_t[:], in_=gt.rearrange("(p t) o -> p (t o)", t=PACK))
+        n4_t = load_list("n4_t", n4)
+
+        b_win = []
+        for t in range(PACK):
+            win = sb("b_win%d" % t, [P, H + PAD], F32)
+            nc.gpsimd.memset(win[:, H:], 0.0)
+            b_win.append(win)
+
+        def gather_scales(name, lst):
+            picked = sb(name + "_picked", [P, S], U8, tag="picked")
+            nc.vector.tensor_copy(picked[:], xs[:].indirect(lst[:]))
+            dealt = sb(name + "_dealt", [P, S], U8)
+            nc.vector.tensor_copy(out=dealt[:].rearrange("p (t m) -> p m t", t=PACK), in_=picked[:].rearrange("p (m t) -> p m t", t=PACK))
+            return dealt
+
+        def gather_words(name, lst):
+            dealt = sb(name, [P, S], U32)
+            nc.vector.tensor_copy(dealt[:].rearrange("p (t m) -> p m t", t=PACK), xw[:].bitcast(U32).indirect(lst[:]))
+            return dealt
+
+        def round_weights(name, raw):
+            grouped = sb(name, [P, HALF, PACK], BF16)
+            nc.scalar.copy(out=grouped[:].rearrange("p (c i) j -> p c j i", i=4), in_=raw[:].rearrange("p j (c i) -> p c j i", i=4))
+            return grouped
+
+        def quantise(codes, scales, grouped):
+            nc.vector.quantize_mx(out=codes.bitcast(FP8X4), scales=scales, in_=grouped)
+
+        def product(acc, l_codes, l_scales, t, r_codes, r_scales):
+            cols = slice(t * P, (t + 1) * P)
+            nc.tensor.matmul_mx(
+                out=acc[:],
+                lhsT=l_codes[:, cols].bitcast(FP8X4),
+                lhsT_scale=l_scales[:, cols],
+                rhs=r_codes[:].bitcast(FP8X4),
+                rhs_scale=r_scales[:],
+                start=True,
+                stop=True,
+            )
+
+        xb = gather_words("xb", two_t)
+        sb_scales = gather_scales("two_s", two_t)
+        wb_codes = sb("wb_codes", [P, H], U32)
+        wb_scales = sb("wb_scales", [P, H], U8)
+        for h in range(2):
+            cols = slice(h * HALF, (h + 1) * HALF)
+            grouped = round_weights("wb_g%d" % h, wb_raw[h])
+            quantise(wb_codes[:, cols], wb_scales[:, cols], grouped[:].rearrange("p c j -> p (c j)"))
+
+        b_ps = []
+        for t in range(PACK):
+            acc = psum.tile([P, H], F32, name="b_ps%d" % t, tag="bank%d" % t)
+            product(acc, xb, sb_scales, t, wb_codes, wb_scales)
+            b_ps.append(acc)
+
+        z2p = sb("z2p", [P, PACK, H], BF16)
+        zp = {}
+        th = [None] * PACK
+        dd = [None] * PACK
+
+        def evac_b(t):
+            if t in EVAC_V:
+                nc.vector.tensor_copy(out=b_win[t][:, :H], in_=b_ps[t][:])
+            else:
+                nc.scalar.copy(out=b_win[t][:, :H], in_=b_ps[t][:])
+
+        def diff(t):
+            g1 = sb("g1_%d" % t, [P, H], F32)
+            nc.scalar.activation(g1[:], b_win[t][:].indirect(n1_t[:]), ACT.Copy, scale=-1.0)
+            d = sb("d_%d" % t, [P, H], F32)
+            if t in N2_S:
+                g2 = sb("g2_%d" % t, [P, H], F32)
+                nc.scalar.activation(g2[:], b_win[t][:].indirect(n2_t[:]), ACT.Copy)
+                nc.vector.tensor_tensor(d[:], g2[:], g1[:], ALU.add)
+            else:
+                nc.vector.tensor_tensor(d[:], b_win[t][:].indirect(n2_t[:]), g1[:], ALU.add)
+            dd[t] = d
+
+        def z2_plane(t):
+            if t in Z2_S:
+                nc.scalar.activation(z2p[:, t, :], b_win[t][:, :H], ACT.Copy, scale=gi_t[:, t : t + 1])
+            else:
+                nc.vector.tensor_scalar(out=z2p[:, t, :], in0=b_win[t][:, :H], scalar1=gi_t[:, t : t + 1], scalar2=None, op0=ALU.mult)
+
+        def tanh(t):
+            th[t] = sb("th_%d" % t, [P, PACK, P], F32)
+            nc.scalar.activation(th[t][:].rearrange("p r m -> p m r"), dd[t][:].rearrange("p (m r) -> p m r", r=PACK), ACT.Tanh, scale=-1.0)
+
+        def z_part(t, r0, r1):
+            nc.vector.scalar_tensor_tensor(
+                out=zp[r0][:, t, : r1 - r0, :],
+                in0=a_ps[t][:].rearrange("p (m r) -> p r m", r=PACK)[:, r0:r1, :],
+                scalar=gt_t[:, t : t + 1],
+                in1=th[t][:, r0:r1, :],
+                op0=ALU.mult,
+                op1=ALU.mult,
+            )
+
+        wa_codes = sb("wa_codes", [P, H], U32)
+        wa_scales = sb("wa_scales", [P, H], U8)
+
+        def wa_half(h):
+            cols = slice(h * HALF, (h + 1) * HALF)
+            grouped = round_weights("wa_g%d" % h, wa_raw[h])
+            quantise(wa_codes[:, cols], wa_scales[:, cols], grouped[:].rearrange("p c j -> p (c j)"))
+
+        a_ps = []
+
+        def a_products():
+            for t in range(PACK):
+                acc = psum.tile([P, H], F32, name="a_ps%d" % t, tag="abank%d" % t)
+                product(acc, xa, sa_scales, t, wa_codes, wa_scales)
+                a_ps.append(acc)
+
+        z2g = sb("z2g", [P, H, PACK], BF16)
+        z2_codes = sb("z2_codes", [P, H], U32)
+        z2_scales = sb("z2_scales", [P, H], U8)
+
+        def z2_finish():
+            nc.vector.tensor_copy(out=z2g[:].rearrange("p (c i) t -> p c t i", i=4), in_=z2p[:].rearrange("p t (c i) -> p c t i", i=4))
+            quantise(z2_codes[:], z2_scales[:], z2g[:].rearrange("p c t -> p (c t)"))
+
+        zg = sb("zg", [P, PACK, P, PACK], BF16)
+        z_codes = sb("z_codes", [P, H], U32)
+        z_scales = sb("z_scales", [P, H], U8)
+        cv_ps = [None] * PACK
+
+        def z_finish(r0, r1):
+            nc.vector.tensor_copy(
+                out=zg[:, r0:r1].rearrange("p r (c i) t -> p (r c) t i", i=4),
+                in_=zp[r0][:, :, : r1 - r0, :].rearrange("p t r (c i) -> p (r c) t i", i=4),
+            )
+            cols = slice(r0 * P, r1 * P)
+            quantise(z_codes[:, cols], z_scales[:, cols], zg[:, r0:r1].rearrange("p r m t -> p (r m t)"))
+            for r in range(r0, r1):
+                cv_ps[r] = psum.tile([P, H], F32, name="cv_ps%d" % r, tag="bank%d" % r)
+                product(cv_ps[r], z_codes, z_scales, r, z2_codes, z2_scales)
+
+        def z_group(r0, r1):
+            zp[r0] = sb("zp%d" % r0, [P, PACK, r1 - r0, P], BF16, tag="zp")
+            for t in range(PACK):
+                z_part(t, r0, r1)
+            z_finish(r0, r1)
+
+        zp[0] = sb("zp0", [P, PACK, FIRST, P], BF16, tag="zp")
+        wa_half(0)
+        evac_b(0)
+        diff(0)
+        xa = gather_words("xa", offs_t)
+        sa_scales = gather_scales("offs_s", offs_t)
+        z2_plane(0)
+        evac_b(1)
+        diff(1)
+        z2_plane(1)
+        wa_half(1)
+        a_products()
+        evac_b(2)
+        diff(2)
+        z2_plane(2)
+        tanh(0)
+        evac_b(3)
+        z2_plane(3)
+        diff(3)
+        tanh(1)
+        z_part(0,0,FIRST)
+        z_part(1,0,FIRST)
+        z2_finish()
+        tanh(2)
+        z_part(2,0,FIRST)
+        tanh(3)
+        z_part(3,0,FIRST)
+        z_finish(0,FIRST)
+
+        out_rows = out_0.rearrange("(p r) c -> p r c", r=PACK)
+        og = sb("og", [P, H, PACK], BF16)
+        cv = [None] * PACK
+        ra = [None] * PACK
+
+        def front(r):
+            cv[r] = sb("cv%d" % r, [P, H], F32)
+            if r == 0:
+                nc.scalar.activation(cv[r][:], cv_ps[r][:], ACT.Copy, scale=0.0625)
+            else:
+                nc.vector.tensor_scalar(out=cv[r][:], in0=cv_ps[r][:], scalar1=0.0625, scalar2=None, op0=ALU.mult)
+            pa = sb("pa%d" % r, [P, W], F32)
+            nc.vector.tensor_copy(pa[:], cv[r][:].indirect(n4_t[:]))
+            old = sb("old%d" % r, [P, W], F32, tag="old", bufs=2)
+            nc.scalar.activation(old[:], cv[r][:].indirect(n3_t[:]), ACT.Copy)
+            tp = sb("tp%d" % r, [P, W], F32)
+            nc.scalar.activation(tp[:], pa[:], ACT.Tanh)
+            ra[r] = sb("ra%d" % r, [P, W], F32)
+            nc.vector.tensor_tensor(ra[r][:], old[:], tp[:], ALU.subtract)
+
+        def back(r):
+            nc.scalar.activation(cv[r][:].indirect(n3_t[:]), ra[r][:], ACT.Copy)
+            nc.sync.dma_start(out=out_rows[:, r, :], in_=cv[r][:])
+            nc.vector.tensor_copy(out=og[:, :, r], in_=cv[r][:])
+
+        front(0)
+        front(1)
+        back(0)
+        z_group(2, 4)
+        front(2)
+        back(1)
+        front(3)
+        back(2)
+        back(3)
+
+        o_codes = sb("o_codes", [P, H], U32)
+        o_scales = sb("o_scales", [P, H], U8)
+        quantise(o_codes[:], o_scales[:], og[:].rearrange("p c r -> p (c r)"))
+        nc.sync.dma_start(out=out_1[0].rearrange("p c r -> p (c r)").bitcast(I32), in_=o_codes[:].bitcast(I32))
+        for q in range(4):
+            eng = nc.scalar if q % 2 else nc.sync
+            eng.dma_start(out=out_2[0, 4 * q : 4 * q + 4, :].bitcast(I32), in_=o_scales[32 * q : 32 * q + 4, :].bitcast(I32))

@@ -2,7 +2,7 @@ from contextlib import ExitStack
 
 import concourse.mybir as mybir
 
-K, T, S, H, W = 512, 2048, 512, 512, 384
+T, S, H, W = 2048, 512, 512, 384
 FLOPS = 3 * 2 * 512 * 512 * 512
 
 F32 = mybir.dt.float32
@@ -19,10 +19,11 @@ P = 128
 PACK = 4
 PAD = 8
 HALF = 256
-EVAC_V = ()
-N2_S = (3,)
-Z2_S = ()
-FIRST = 2
+PAIR = 2
+B_BANKS = (("bank0",), ("bank1",), ("bank0",), ("bank1",))
+CV_BANKS = (("bank2", "bank3"), ("bank0",), ("bank1",), ("bank2",))
+HALVES = (slice(0, HALF), slice(HALF, H))
+WHOLE = (slice(0, H),)
 
 
 def tile_picked_momtjointbktanh_none_po_kernel(
@@ -33,41 +34,46 @@ def tile_picked_momtjointbktanh_none_po_kernel(
         keep = ctx.enter_context(tc.tile_pool(name="keep", bufs=1))
         psum = ctx.enter_context(tc.psum_pool(name="psum", bufs=1))
 
-        def sb(name, shape, dtype, tag=None, bufs=1):
-            return keep.tile(shape, dtype, name=name, tag=tag or name, bufs=bufs, align_bytes=64)
+        def sb(name, shape, dtype, tag=None):
+            return keep.tile(shape, dtype, name=name, tag=tag or name, align_bytes=64)
 
         def load_list(name, src):
-            t = keep.tile(list(src.shape), U16, name=name)
-            nc.sync.dma_start(t[:], src)
-            return t
+            lst = keep.tile(list(src.shape), U16, name=name)
+            nc.sync.dma_start(lst[:], src)
+            return lst
 
-        wb_rows = wb.rearrange("(p j) n -> p j n", j=PACK)
-        wa_rows = wa.rearrange("(p j) n -> p j n", j=PACK)
-
-        def load_half(name, rows, h):
+        def load_half(name, w, h):
             raw = sb(name, [P, PACK, HALF], F32)
-            nc.sync.dma_start(out=raw[:], in_=rows[:, :, h * HALF : (h + 1) * HALF])
+            nc.sync.dma_start(out=raw[:], in_=w.rearrange("(p j) n -> p j n", j=PACK)[:, :, h * HALF : (h + 1) * HALF])
             return raw
+
+        def load_gain(name, g):
+            gain = sb(name, [P, PACK], F32)
+            nc.sync.dma_start(out=gain[:], in_=g.rearrange("(p t) o -> p (t o)", t=PACK))
+            return gain
+
+        def load_words():
+            words = sb("xw", [P, T], I32)
+            nc.sync.dma_start(out=words[:], in_=x_words[0].rearrange("p c r -> p (c r)").bitcast(I32))
+            return words
 
         xs = sb("xs", [P, T], U8)
         nc.gpsimd.memset(xs[:].bitcast(I32), 0)
-        for q in range(4):
-            nc.scalar.dma_start(out=xs[32 * q : 32 * q + 4, :].bitcast(I32), in_=x_scales[0, 4 * q : 4 * q + 4, :].bitcast(I32))
         two_t = load_list("two_t", two)
         offs_t = load_list("offs_t", offs)
+        for q in range(4):
+            queue = nc.sync if q % 2 else nc.scalar
+            queue.dma_start(out=xs[32 * q : 32 * q + 4, :].bitcast(I32), in_=x_scales[0, 4 * q : 4 * q + 4, :].bitcast(I32))
+        xw = load_words()
+        wb_raw = [load_half("wb_raw0", wb, 0)]
         n1_t = load_list("n1_t", n1)
-        xw = sb("xw", [P, T], I32)
-        nc.sync.dma_start(out=xw[:], in_=x_words[0].rearrange("p c r -> p (c r)").bitcast(I32))
         n2_t = load_list("n2_t", n2)
+        gi_t = load_gain("gi_t", gi)
+        wb_raw.append(load_half("wb_raw1", wb, 1))
+        wa_raw = [load_half("wa_raw%d" % h, wa, h) for h in range(2)]
+        gt_t = load_gain("gt_t", gt)
         n3_t = load_list("n3_t", n3)
-        wb_raw = [load_half("wb_raw%d" % h, wb_rows, h) for h in range(2)]
-        wa_raw = [load_half("wa_raw%d" % h, wa_rows, h) for h in range(2)]
-        gi_t = sb("gi_t", [P, PACK], F32)
-        nc.sync.dma_start(out=gi_t[:], in_=gi.rearrange("(p t) o -> p (t o)", t=PACK))
-        gt_t = sb("gt_t", [P, PACK], F32)
-        nc.sync.dma_start(out=gt_t[:], in_=gt.rearrange("(p t) o -> p (t o)", t=PACK))
         n4_t = load_list("n4_t", n4)
-
         b_win = []
         for t in range(PACK):
             win = sb("b_win%d" % t, [P, H + PAD], F32)
@@ -86,198 +92,221 @@ def tile_picked_momtjointbktanh_none_po_kernel(
             nc.vector.tensor_copy(dealt[:].rearrange("p (t m) -> p m t", t=PACK), xw[:].bitcast(U32).indirect(lst[:]))
             return dealt
 
-        def round_weights(name, raw):
-            grouped = sb(name, [P, HALF, PACK], BF16)
-            nc.scalar.copy(out=grouped[:].rearrange("p (c i) j -> p c j i", i=4), in_=raw[:].rearrange("p j (c i) -> p c j i", i=4))
-            return grouped
-
         def quantise(codes, scales, grouped):
             nc.vector.quantize_mx(out=codes.bitcast(FP8X4), scales=scales, in_=grouped)
 
-        def product(acc, l_codes, l_scales, t, r_codes, r_scales):
+        def weight_half(name, raw, h, codes, scales, copy):
+            grouped = sb(name, [P, HALF, PACK], BF16)
+            copy(out=grouped[:].rearrange("p (c i) j -> p c j i", i=4), in_=raw[:].rearrange("p j (c i) -> p c j i", i=4))
+            cols = slice(h * HALF, (h + 1) * HALF)
+            quantise(codes[:, cols], scales[:, cols], grouped[:].rearrange("p c j -> p (c j)"))
+
+        def product(name, bank, l_codes, l_scales, t, r_codes, r_scales, moving=slice(0, H)):
+            acc = psum.tile([P, moving.stop - moving.start], F32, name=name, tag=bank)
             cols = slice(t * P, (t + 1) * P)
             nc.tensor.matmul_mx(
                 out=acc[:],
                 lhsT=l_codes[:, cols].bitcast(FP8X4),
                 lhsT_scale=l_scales[:, cols],
-                rhs=r_codes[:].bitcast(FP8X4),
-                rhs_scale=r_scales[:],
+                rhs=r_codes[:, moving].bitcast(FP8X4),
+                rhs_scale=r_scales[:, moving],
                 start=True,
                 stop=True,
             )
+            return acc
 
-        xb = gather_words("xb", two_t)
-        sb_scales = gather_scales("two_s", two_t)
+        xb_scales = gather_scales("two_s", two_t)
+        xa_scales = gather_scales("offs_s", offs_t)
+        xb_codes = gather_words("xb", two_t)
         wb_codes = sb("wb_codes", [P, H], U32)
         wb_scales = sb("wb_scales", [P, H], U8)
         for h in range(2):
-            cols = slice(h * HALF, (h + 1) * HALF)
-            grouped = round_weights("wb_g%d" % h, wb_raw[h])
-            quantise(wb_codes[:, cols], wb_scales[:, cols], grouped[:].rearrange("p c j -> p (c j)"))
+            weight_half("wb_g%d" % h, wb_raw[h], h, wb_codes, wb_scales, nc.scalar.copy)
+        b_ps = {}
 
-        b_ps = []
-        for t in range(PACK):
-            acc = psum.tile([P, H], F32, name="b_ps%d" % t, tag="bank%d" % t)
-            product(acc, xb, sb_scales, t, wb_codes, wb_scales)
-            b_ps.append(acc)
+        def b_product(t):
+            parts = WHOLE
+            b_ps[t] = [
+                (cols, product("b_ps%d_%d" % (t, i), B_BANKS[t][i], xb_codes, xb_scales, t, wb_codes, wb_scales, cols))
+                for i, cols in enumerate(parts)
+            ]
 
-        z2p = sb("z2p", [P, PACK, H], BF16)
-        zp = {}
-        th = [None] * PACK
-        dd = [None] * PACK
+        b_product(0)
+        b_product(1)
+
+        xa_codes = gather_words("xa", offs_t)
+        wa_codes = sb("wa_codes", [P, H], U32)
+        wa_scales = sb("wa_scales", [P, H], U8)
+        weight_half("wa_g0", wa_raw[0], 0, wa_codes, wa_scales, nc.scalar.copy)
+        weight_half("wa_g1", wa_raw[1], 1, wa_codes, wa_scales, nc.vector.tensor_copy)
+        a_ps = [product("a_ps%d" % t, "abank%d" % t, xa_codes, xa_scales, t, wa_codes, wa_scales) for t in range(PACK)]
+
+        z2_pairs = sb("z2_pairs", [P, 2, H, 2], BF16)
+        diff = []
 
         def evac_b(t):
-            if t in EVAC_V:
-                nc.vector.tensor_copy(out=b_win[t][:, :H], in_=b_ps[t][:])
-            else:
-                nc.scalar.copy(out=b_win[t][:, :H], in_=b_ps[t][:])
+            if t not in b_ps:
+                b_product(t)
+            copy = nc.vector.tensor_copy if t in (1,) else nc.scalar.copy
+            for cols, acc in b_ps[t]:
+                copy(out=b_win[t][:, cols], in_=acc[:])
 
-        def diff(t):
+        def z2_plane(t):
+            nc.vector.tensor_scalar(
+                out=z2_pairs[:, t // 2, :, t % 2], in0=b_win[t][:, :H], scalar1=gi_t[:, t : t + 1], scalar2=None, op0=ALU.mult
+            )
+
+        def difference(t):
             g1 = sb("g1_%d" % t, [P, H], F32)
             nc.scalar.activation(g1[:], b_win[t][:].indirect(n1_t[:]), ACT.Copy, scale=-1.0)
             d = sb("d_%d" % t, [P, H], F32)
-            if t in N2_S:
+            if t in (3,):
                 g2 = sb("g2_%d" % t, [P, H], F32)
                 nc.scalar.activation(g2[:], b_win[t][:].indirect(n2_t[:]), ACT.Copy)
                 nc.vector.tensor_tensor(d[:], g2[:], g1[:], ALU.add)
             else:
                 nc.vector.tensor_tensor(d[:], b_win[t][:].indirect(n2_t[:]), g1[:], ALU.add)
-            dd[t] = d
+            diff.append(d)
 
-        def z2_plane(t):
-            if t in Z2_S:
-                nc.scalar.activation(z2p[:, t, :], b_win[t][:, :H], ACT.Copy, scale=gi_t[:, t : t + 1])
-            else:
-                nc.vector.tensor_scalar(out=z2p[:, t, :], in0=b_win[t][:, :H], scalar1=gi_t[:, t : t + 1], scalar2=None, op0=ALU.mult)
-
-        def tanh(t):
-            th[t] = sb("th_%d" % t, [P, PACK, P], F32)
-            nc.scalar.activation(th[t][:].rearrange("p r m -> p m r"), dd[t][:].rearrange("p (m r) -> p m r", r=PACK), ACT.Tanh, scale=-1.0)
-
-        def z_part(t, r0, r1):
-            nc.vector.scalar_tensor_tensor(
-                out=zp[r0][:, t, : r1 - r0, :],
-                in0=a_ps[t][:].rearrange("p (m r) -> p r m", r=PACK)[:, r0:r1, :],
-                scalar=gt_t[:, t : t + 1],
-                in1=th[t][:, r0:r1, :],
-                op0=ALU.mult,
-                op1=ALU.mult,
-            )
-
-        wa_codes = sb("wa_codes", [P, H], U32)
-        wa_scales = sb("wa_scales", [P, H], U8)
-
-        def wa_half(h):
-            cols = slice(h * HALF, (h + 1) * HALF)
-            grouped = round_weights("wa_g%d" % h, wa_raw[h])
-            quantise(wa_codes[:, cols], wa_scales[:, cols], grouped[:].rearrange("p c j -> p (c j)"))
-
-        a_ps = []
-
-        def a_products():
-            for t in range(PACK):
-                acc = psum.tile([P, H], F32, name="a_ps%d" % t, tag="abank%d" % t)
-                product(acc, xa, sa_scales, t, wa_codes, wa_scales)
-                a_ps.append(acc)
-
-        z2g = sb("z2g", [P, H, PACK], BF16)
+        z2_grouped = sb("z2g", [P, H, PACK], BF16)
         z2_codes = sb("z2_codes", [P, H], U32)
         z2_scales = sb("z2_scales", [P, H], U8)
 
         def z2_finish():
-            nc.vector.tensor_copy(out=z2g[:].rearrange("p (c i) t -> p c t i", i=4), in_=z2p[:].rearrange("p t (c i) -> p c t i", i=4))
-            quantise(z2_codes[:], z2_scales[:], z2g[:].rearrange("p c t -> p (c t)"))
-
-        zg = sb("zg", [P, PACK, P, PACK], BF16)
-        z_codes = sb("z_codes", [P, H], U32)
-        z_scales = sb("z_scales", [P, H], U8)
-        cv_ps = [None] * PACK
-
-        def z_finish(r0, r1):
             nc.vector.tensor_copy(
-                out=zg[:, r0:r1].rearrange("p r (c i) t -> p (r c) t i", i=4),
-                in_=zp[r0][:, :, : r1 - r0, :].rearrange("p t r (c i) -> p (r c) t i", i=4),
+                out=z2_grouped[:].bitcast(F32), in_=z2_pairs[:].bitcast(F32).rearrange("p u c o -> p c (u o)")
             )
-            cols = slice(r0 * P, r1 * P)
-            quantise(z_codes[:, cols], z_scales[:, cols], zg[:, r0:r1].rearrange("p r m t -> p (r m t)"))
-            for r in range(r0, r1):
-                cv_ps[r] = psum.tile([P, H], F32, name="cv_ps%d" % r, tag="bank%d" % r)
-                product(cv_ps[r], z_codes, z_scales, r, z2_codes, z2_scales)
+            quantise(z2_codes[:], z2_scales[:], z2_grouped[:].rearrange("p c t -> p (c t)"))
 
-        def z_group(r0, r1):
-            zp[r0] = sb("zp%d" % r0, [P, PACK, r1 - r0, P], BF16, tag="zp")
-            for t in range(PACK):
-                z_part(t, r0, r1)
-            z_finish(r0, r1)
-
-        zp[0] = sb("zp0", [P, PACK, FIRST, P], BF16, tag="zp")
-        wa_half(0)
         evac_b(0)
-        diff(0)
-        xa = gather_words("xa", offs_t)
-        sa_scales = gather_scales("offs_s", offs_t)
         z2_plane(0)
         evac_b(1)
-        diff(1)
         z2_plane(1)
-        wa_half(1)
-        a_products()
+        difference(0)
+        difference(1)
         evac_b(2)
-        diff(2)
-        z2_plane(2)
-        tanh(0)
         evac_b(3)
+        difference(2)
+        z2_plane(2)
         z2_plane(3)
-        diff(3)
-        tanh(1)
-        z_part(0,0,FIRST)
-        z_part(1,0,FIRST)
+        difference(3)
         z2_finish()
-        tanh(2)
-        z_part(2,0,FIRST)
-        tanh(3)
-        z_part(3,0,FIRST)
-        z_finish(0,FIRST)
+
+        z_codes = sb("z_codes", [P, H], U32)
+        z_scales = sb("z_scales", [P, H], U8)
+        cv_ps = []
+
+        def z_pair(u, th_tag):
+            rs = slice(PAIR * u, PAIR * (u + 1))
+            th = sb("th%d" % u, [P, PACK, PAIR, P], F32, tag=th_tag)
+            planes = sb("zp%d" % u, [P, PACK, PAIR, P], BF16, tag="zp")
+            for t in range(PACK):
+                nc.scalar.activation(
+                    th[:, t].rearrange("p r m -> p m r"), diff[t][:].rearrange("p (m r) -> p m r", r=PACK)[:, :, rs], ACT.Tanh, scale=-1.0
+                )
+                nc.vector.scalar_tensor_tensor(
+                    out=planes[:, t],
+                    in0=a_ps[t][:].rearrange("p (m r) -> p r m", r=PACK)[:, rs, :],
+                    scalar=gt_t[:, t : t + 1],
+                    in1=th[:, t],
+                    op0=ALU.mult,
+                    op1=ALU.mult,
+                )
+            grouped = sb("zg%d" % u, [P, PAIR * P, PACK], BF16)
+            nc.vector.tensor_copy(
+                out=grouped[:].rearrange("p (c i) t -> p c t i", i=4),
+                in_=planes[:].rearrange("p t r (c i) -> p (r c) t i", i=4),
+            )
+            cols = slice(u * HALF, (u + 1) * HALF)
+            quantise(z_codes[:, cols], z_scales[:, cols], grouped[:].rearrange("p c t -> p (c t)"))
+            for r in range(PAIR * u, PAIR * (u + 1)):
+                parts = HALVES if r == 0 else WHOLE
+                cv_ps.append([
+                    (cols, product("cv_ps%d_%d" % (r, i), CV_BANKS[r][i], z_codes, z_scales, r, z2_codes, z2_scales, cols))
+                    for i, cols in enumerate(parts)
+                ])
 
         out_rows = out_0.rearrange("(p r) c -> p r c", r=PACK)
-        og = sb("og", [P, H, PACK], BF16)
-        cv = [None] * PACK
-        ra = [None] * PACK
+        cv, pa, old, tp, ra = {}, {}, {}, {}, {}
 
-        def front(r):
-            cv[r] = sb("cv%d" % r, [P, H], F32)
-            if r == 0:
-                nc.scalar.activation(cv[r][:], cv_ps[r][:], ACT.Copy, scale=0.0625)
-            else:
-                nc.vector.tensor_scalar(out=cv[r][:], in0=cv_ps[r][:], scalar1=0.0625, scalar2=None, op0=ALU.mult)
-            pa = sb("pa%d" % r, [P, W], F32)
-            nc.vector.tensor_copy(pa[:], cv[r][:].indirect(n4_t[:]))
-            old = sb("old%d" % r, [P, W], F32, tag="old", bufs=2)
-            nc.scalar.activation(old[:], cv[r][:].indirect(n3_t[:]), ACT.Copy)
-            tp = sb("tp%d" % r, [P, W], F32)
-            nc.scalar.activation(tp[:], pa[:], ACT.Tanh)
-            ra[r] = sb("ra%d" % r, [P, W], F32)
-            nc.vector.tensor_tensor(ra[r][:], old[:], tp[:], ALU.subtract)
+        def evac(r, on_scalar=False, tag=None):
+            cv[r] = sb("cv%d" % r, [P, H], F32, tag=tag)
+            for cols, acc in cv_ps[r]:
+                if on_scalar:
+                    nc.scalar.activation(cv[r][:, cols], acc[:], ACT.Copy, scale=0.0625)
+                else:
+                    nc.vector.tensor_scalar(out=cv[r][:, cols], in0=acc[:], scalar1=0.0625, scalar2=None, op0=ALU.mult)
 
-        def back(r):
-            nc.scalar.activation(cv[r][:].indirect(n3_t[:]), ra[r][:], ACT.Copy)
+        def g_pa(r, tag=None):
+            pa[r] = sb("pa%d" % r, [P, W], F32, tag=tag)
+            nc.vector.tensor_copy(pa[r][:], cv[r][:].indirect(n4_t[:]))
+
+        def g_old(r, tag=None):
+            if r not in old:
+                old[r] = sb("old%d" % r, [P, W], F32, tag=tag)[:]
+            nc.scalar.activation(old[r], cv[r][:].indirect(n3_t[:]), ACT.Copy)
+
+        def t_pa(r, tag=None):
+            tp[r] = sb("tp%d" % r, [P, W], F32, tag=tag)
+            nc.scalar.activation(tp[r][:], pa[r][:], ACT.Tanh)
+
+        def hold(r, tag):
+            held = sb("held%d" % r, [P, 2, W], F32, tag=tag)
+            old[r] = held[:, 0, :]
+            ra[r - 1] = held[:, 1, :]
+
+        def sub(r, tag=None):
+            if r not in ra:
+                ra[r] = sb("ra%d" % r, [P, W], F32, tag=tag)[:]
+            nc.vector.tensor_tensor(ra[r], old[r], tp[r][:], ALU.subtract)
+
+        def put(r):
+            nc.scalar.activation(cv[r][:].indirect(n3_t[:]), ra[r], ACT.Copy)
             nc.sync.dma_start(out=out_rows[:, r, :], in_=cv[r][:])
+
+        z_pair(0, "g1_2")
+        evac(0, True)
+        g_pa(0)
+        g_old(0)
+        t_pa(0)
+        z_pair(1, "g1_3")
+        sub(0)
+        evac(1, tag="zp")
+        g_pa(1)
+        g_old(1)
+        put(0)
+        t_pa(1)
+        evac(2)
+        g_pa(2)
+        t_pa(2)
+        hold(2, "pa2")
+        g_old(2)
+        sub(1)
+        put(1)
+        evac(3)
+        g_pa(3)
+        t_pa(3, "tp1")
+        hold(3, "pa3")
+        g_old(3)
+        sub(2)
+        put(2)
+        sub(3)
+        put(3)
+
+        last = PACK - 1
+        og = sb("og", [P, H, PACK], BF16, tag="old1")
+        for r in range(last):
             nc.vector.tensor_copy(out=og[:, :, r], in_=cv[r][:])
-
-        front(0)
-        front(1)
-        back(0)
-        z_group(2, 4)
-        front(2)
-        back(1)
-        front(3)
-        back(2)
-        back(3)
-
         o_codes = sb("o_codes", [P, H], U32)
         o_scales = sb("o_scales", [P, H], U8)
-        quantise(o_codes[:], o_scales[:], og[:].rearrange("p c r -> p (c r)"))
-        nc.sync.dma_start(out=out_1[0].rearrange("p c r -> p (c r)").bitcast(I32), in_=o_codes[:].bitcast(I32))
+        out_words = out_1[0].rearrange("p c r -> p (c r)").bitcast(I32)
+        for h in range(2):
+            cols = slice(h * HALF, (h + 1) * HALF)
+            nc.vector.tensor_copy(out=og[:, cols, last], in_=cv[last][:, cols])
+        for h in range(2):
+            cols = slice(h * HALF, (h + 1) * HALF)
+            quantise(o_codes[:, cols], o_scales[:, cols], og[:, cols, :].rearrange("p c r -> p (c r)"))
+            nc.sync.dma_start(out=out_words[:, cols], in_=o_codes[:, cols].bitcast(I32))
         for q in range(4):
-            eng = nc.scalar if q % 2 else nc.sync
+            eng = nc.sync if q % 2 else nc.scalar
             eng.dma_start(out=out_2[0, 4 * q : 4 * q + 4, :].bitcast(I32), in_=o_scales[32 * q : 32 * q + 4, :].bitcast(I32))

@@ -1,6 +1,7 @@
 from contextlib import ExitStack
 
 import concourse.mybir as mybir
+from concourse.masks import make_identity
 
 T, S, H, W = 2048, 512, 512, 384
 FLOPS = 3 * 2 * 512 * 512 * 512
@@ -17,13 +18,16 @@ ALU = mybir.AluOpType
 
 P = 128
 PACK = 4
-PAD = 8
-HALF = 256
+RUN = 8
+QUADRANTS = 4
+SPARE = 8
 PAIR = 2
-B_BANKS = (("bank0",), ("bank1",), ("bank0",), ("bank1",))
-CV_BANKS = (("bank2", "bank3"), ("bank0",), ("bank1",), ("bank2",))
-HALVES = (slice(0, HALF), slice(HALF, H))
-WHOLE = (slice(0, H),)
+LAST = PACK - 1
+ALL = slice(0, H)
+HALVES = (slice(0, H // 2), slice(H // 2, H))
+WA_SCALAR, WA_VECTOR = slice(0, 128), slice(128, H)
+N2_ON_SCALAR = (2, 3)
+B_OUT_ON_VECTOR = 1
 
 
 def tile_picked_momtjointbktanh_none_po_kernel(
@@ -34,80 +38,89 @@ def tile_picked_momtjointbktanh_none_po_kernel(
         keep = ctx.enter_context(tc.tile_pool(name="keep", bufs=1))
         psum = ctx.enter_context(tc.psum_pool(name="psum", bufs=1))
 
-        def sb(name, shape, dtype, tag=None):
-            return keep.tile(shape, dtype, name=name, tag=tag or name, align_bytes=64)
+        def sb(name, shape, dtype, reuse=None):
+            return keep.tile(shape, dtype, name=name, tag=reuse or name, align_bytes=64)
+
+        def width(cols):
+            return cols.stop - cols.start
 
         def load_list(name, src):
-            lst = keep.tile(list(src.shape), U16, name=name)
-            nc.sync.dma_start(lst[:], src)
-            return lst
+            offsets = keep.tile(list(src.shape), U16, name=name)
+            nc.sync.dma_start(offsets[:], src)
+            return offsets
 
-        def load_half(name, w, h):
-            raw = sb(name, [P, PACK, HALF], F32)
-            nc.sync.dma_start(out=raw[:], in_=w.rearrange("(p j) n -> p j n", j=PACK)[:, :, h * HALF : (h + 1) * HALF])
+        def load_weight(name, w, cols):
+            raw = sb(name, [P, PACK, width(cols)], F32)
+            nc.sync.dma_start(out=raw[:], in_=w.rearrange("(p j) n -> p j n", j=PACK)[:, :, cols])
             return raw
 
-        def load_gain(name, g):
-            gain = sb(name, [P, PACK], F32)
-            nc.sync.dma_start(out=gain[:], in_=g.rearrange("(p t) o -> p (t o)", t=PACK))
-            return gain
+        x_scale_table = sb("x_scale_table", [P, T], U8)
+        nc.gpsimd.memset(x_scale_table[:].bitcast(I32), 0)
+        gain_rows = sb("gain_rows", [P, P], F32)
+        nc.gpsimd.memset(gain_rows[:], 0.0)
+        identity = sb("identity", [P, P], F32)
+        make_identity(nc, identity[:])
 
-        def load_words():
-            words = sb("xw", [P, T], I32)
-            nc.sync.dma_start(out=words[:], in_=x_words[0].rearrange("p c r -> p (c r)").bitcast(I32))
-            return words
-
-        xs = sb("xs", [P, T], U8)
-        nc.gpsimd.memset(xs[:].bitcast(I32), 0)
-        two_t = load_list("two_t", two)
-        offs_t = load_list("offs_t", offs)
-        for q in range(4):
+        two_list = load_list("two_list", two)
+        offs_list = load_list("offs_list", offs)
+        for q in range(QUADRANTS):
             queue = nc.sync if q % 2 else nc.scalar
-            queue.dma_start(out=xs[32 * q : 32 * q + 4, :].bitcast(I32), in_=x_scales[0, 4 * q : 4 * q + 4, :].bitcast(I32))
-        xw = load_words()
-        wb_raw = [load_half("wb_raw0", wb, 0)]
-        n1_t = load_list("n1_t", n1)
-        n2_t = load_list("n2_t", n2)
-        gi_t = load_gain("gi_t", gi)
-        wb_raw.append(load_half("wb_raw1", wb, 1))
-        wa_raw = [load_half("wa_raw%d" % h, wa, h) for h in range(2)]
-        gt_t = load_gain("gt_t", gt)
-        n3_t = load_list("n3_t", n3)
-        n4_t = load_list("n4_t", n4)
-        b_win = []
-        for t in range(PACK):
-            win = sb("b_win%d" % t, [P, H + PAD], F32)
-            nc.gpsimd.memset(win[:, H:], 0.0)
-            b_win.append(win)
+            queue.dma_start(
+                out=x_scale_table[32 * q : 32 * q + 4, :].bitcast(I32), in_=x_scales[0, 4 * q : 4 * q + 4, :].bitcast(I32)
+            )
+        for first_row, gain in ((0, gi), (PACK, gt)):
+            nc.scalar.dma_start(
+                out=gain_rows[first_row : first_row + PACK, :].rearrange("t (g e) -> t g e", e=RUN),
+                in_=gain.rearrange("(g t e) o -> t g (e o)", t=PACK, e=RUN),
+            )
+        wb_raw = [load_weight("wb_raw%d" % h, wb, cols) for h, cols in enumerate(HALVES)]
+        x_word_table = sb("x_word_table", [P, T], I32)
+        nc.sync.dma_start(out=x_word_table[:], in_=x_words[0].rearrange("p c j -> p (c j)").bitcast(I32))
+        wa_raw_scalar = load_weight("wa_raw_scalar", wa, WA_SCALAR)
+        n1_list = load_list("n1_list", n1)
+        n2_list = load_list("n2_list", n2)
+        wa_raw_vector = load_weight("wa_raw_vector", wa, WA_VECTOR)
+        n3_list = load_list("n3_list", n3)
+        n4_list = load_list("n4_list", n4)
 
-        def gather_scales(name, lst):
-            picked = sb(name + "_picked", [P, S], U8, tag="picked")
-            nc.vector.tensor_copy(picked[:], xs[:].indirect(lst[:]))
-            dealt = sb(name + "_dealt", [P, S], U8)
-            nc.vector.tensor_copy(out=dealt[:].rearrange("p (t m) -> p m t", t=PACK), in_=picked[:].rearrange("p (m t) -> p m t", t=PACK))
+        b_tiles = []
+        for t in range(PACK):
+            b_tile = sb("b%d" % t, [P, H + SPARE], F32)
+            nc.gpsimd.memset(b_tile[:, H:], 0.0)
+            b_tiles.append(b_tile)
+
+        def gather_scales(name, offsets):
+            picked = sb(name + "_picked", [P, S], U8, reuse="picked_scales")
+            nc.vector.tensor_copy(picked[:], x_scale_table[:].indirect(offsets[:]))
+            dealt = sb(name, [P, S], U8)
+            nc.vector.tensor_copy(
+                out=dealt[:].bitcast(I32).rearrange("p (t g w) -> p t g w", t=PACK, w=RUN // 4),
+                in_=picked[:].bitcast(I32).rearrange("p (g t w) -> p t g w", t=PACK, w=RUN // 4),
+            )
             return dealt
 
-        def gather_words(name, lst):
+        def gather_words(name, offsets):
             dealt = sb(name, [P, S], U32)
-            nc.vector.tensor_copy(dealt[:].rearrange("p (t m) -> p m t", t=PACK), xw[:].bitcast(U32).indirect(lst[:]))
+            nc.vector.tensor_copy(
+                dealt[:].rearrange("p (t g e) -> p g t e", t=PACK, e=RUN), x_word_table[:].bitcast(U32).indirect(offsets[:])
+            )
             return dealt
 
         def quantise(codes, scales, grouped):
             nc.vector.quantize_mx(out=codes.bitcast(FP8X4), scales=scales, in_=grouped)
 
-        def weight_half(name, raw, h, codes, scales, copy):
-            grouped = sb(name, [P, HALF, PACK], BF16)
+        def quantise_weight(name, raw, cols, codes, scales, copy):
+            grouped = sb(name, [P, width(cols), PACK], BF16)
             copy(out=grouped[:].rearrange("p (c i) j -> p c j i", i=4), in_=raw[:].rearrange("p j (c i) -> p c j i", i=4))
-            cols = slice(h * HALF, (h + 1) * HALF)
             quantise(codes[:, cols], scales[:, cols], grouped[:].rearrange("p c j -> p (c j)"))
 
-        def product(name, bank, l_codes, l_scales, t, r_codes, r_scales, moving=slice(0, H)):
-            acc = psum.tile([P, moving.stop - moving.start], F32, name=name, tag=bank)
-            cols = slice(t * P, (t + 1) * P)
+        def product(name, bank, l_codes, l_scales, tile, r_codes, r_scales, moving):
+            acc = psum.tile([P, width(moving)], F32, name=name, tag="bank%d" % bank)
+            stationary = slice(tile * P, (tile + 1) * P)
             nc.tensor.matmul_mx(
                 out=acc[:],
-                lhsT=l_codes[:, cols].bitcast(FP8X4),
-                lhsT_scale=l_scales[:, cols],
+                lhsT=l_codes[:, stationary].bitcast(FP8X4),
+                lhsT_scale=l_scales[:, stationary],
                 rhs=r_codes[:, moving].bitcast(FP8X4),
                 rhs_scale=r_scales[:, moving],
                 start=True,
@@ -115,198 +128,196 @@ def tile_picked_momtjointbktanh_none_po_kernel(
             )
             return acc
 
-        xb_scales = gather_scales("two_s", two_t)
-        xa_scales = gather_scales("offs_s", offs_t)
-        xb_codes = gather_words("xb", two_t)
+        gain_psum = psum.tile([P, P], F32, name="gain_psum", tag="bank2")
+        nc.tensor.transpose(gain_psum[:], gain_rows[:], identity[:])
+
+        xb_scales = gather_scales("xb_scales", two_list)
+        xa_scales = gather_scales("xa_scales", offs_list)
+        xb_codes = gather_words("xb_codes", two_list)
         wb_codes = sb("wb_codes", [P, H], U32)
         wb_scales = sb("wb_scales", [P, H], U8)
-        for h in range(2):
-            weight_half("wb_g%d" % h, wb_raw[h], h, wb_codes, wb_scales, nc.scalar.copy)
-        b_ps = {}
+        for h, cols in enumerate(HALVES):
+            quantise_weight("wb_grouped%d" % h, wb_raw[h], cols, wb_codes, wb_scales, nc.scalar.copy)
 
         def b_product(t):
-            parts = WHOLE
-            b_ps[t] = [
-                (cols, product("b_ps%d_%d" % (t, i), B_BANKS[t][i], xb_codes, xb_scales, t, wb_codes, wb_scales, cols))
-                for i, cols in enumerate(parts)
-            ]
+            return product("b_psum%d" % t, t % 2, xb_codes, xb_scales, t, wb_codes, wb_scales, ALL)
 
-        b_product(0)
-        b_product(1)
+        b_psum = [b_product(0), b_product(1)]
 
-        xa_codes = gather_words("xa", offs_t)
+        xa_codes = gather_words("xa_codes", offs_list)
         wa_codes = sb("wa_codes", [P, H], U32)
         wa_scales = sb("wa_scales", [P, H], U8)
-        weight_half("wa_g0", wa_raw[0], 0, wa_codes, wa_scales, nc.scalar.copy)
-        weight_half("wa_g1", wa_raw[1], 1, wa_codes, wa_scales, nc.vector.tensor_copy)
-        a_ps = [product("a_ps%d" % t, "abank%d" % t, xa_codes, xa_scales, t, wa_codes, wa_scales) for t in range(PACK)]
+        quantise_weight("wa_grouped_scalar", wa_raw_scalar, WA_SCALAR, wa_codes, wa_scales, nc.scalar.copy)
+        gains = sb("gains", [P, 2 * PACK], F32, reuse="wa_raw_scalar")
+        nc.scalar.copy(out=gains[:], in_=gain_psum[:, : 2 * PACK])
+        gi_by_tile, gt_by_tile = gains[:, :PACK], gains[:, PACK:]
+        quantise_weight("wa_grouped_vector", wa_raw_vector, WA_VECTOR, wa_codes, wa_scales, nc.vector.tensor_copy)
+        a_psum = [product("a_psum%d" % t, PACK + t, xa_codes, xa_scales, t, wa_codes, wa_scales, ALL) for t in range(PACK)]
 
         z2_pairs = sb("z2_pairs", [P, 2, H, 2], BF16)
-        diff = []
+        neg_diff = []
 
-        def evac_b(t):
-            if t not in b_ps:
-                b_product(t)
-            copy = nc.vector.tensor_copy if t in (1,) else nc.scalar.copy
-            for cols, acc in b_ps[t]:
-                copy(out=b_win[t][:, cols], in_=acc[:])
+        def copy_b_out(t):
+            copy = nc.vector.tensor_copy if t == B_OUT_ON_VECTOR else nc.scalar.copy
+            copy(out=b_tiles[t][:, :H], in_=b_psum[t][:])
 
-        def z2_plane(t):
+        def scale_z2(t):
             nc.vector.tensor_scalar(
-                out=z2_pairs[:, t // 2, :, t % 2], in0=b_win[t][:, :H], scalar1=gi_t[:, t : t + 1], scalar2=None, op0=ALU.mult
+                out=z2_pairs[:, t // 2, :, t % 2], in0=b_tiles[t][:, :H], scalar1=gi_by_tile[:, t : t + 1], scalar2=None, op0=ALU.mult
             )
 
         def difference(t):
-            g1 = sb("g1_%d" % t, [P, H], F32)
-            nc.scalar.activation(g1[:], b_win[t][:].indirect(n1_t[:]), ACT.Copy, scale=-1.0)
-            d = sb("d_%d" % t, [P, H], F32)
-            if t in (3,):
-                g2 = sb("g2_%d" % t, [P, H], F32)
-                nc.scalar.activation(g2[:], b_win[t][:].indirect(n2_t[:]), ACT.Copy)
-                nc.vector.tensor_tensor(d[:], g2[:], g1[:], ALU.add)
+            neg_n1 = sb("neg_n1_%d" % t, [P, H], F32)
+            nc.scalar.activation(neg_n1[:], b_tiles[t][:].indirect(n1_list[:]), ACT.Copy, scale=-1.0)
+            diff = sb("neg_diff%d" % t, [P, H], F32, reuse="z2_grouped0" if t == LAST else None)
+            if t in N2_ON_SCALAR:
+                at_n2 = sb("at_n2_%d" % t, [P, H], F32)
+                nc.scalar.activation(at_n2[:], b_tiles[t][:].indirect(n2_list[:]), ACT.Copy)
+                nc.vector.tensor_tensor(diff[:], at_n2[:], neg_n1[:], ALU.add)
             else:
-                nc.vector.tensor_tensor(d[:], b_win[t][:].indirect(n2_t[:]), g1[:], ALU.add)
-            diff.append(d)
+                nc.vector.tensor_tensor(diff[:], b_tiles[t][:].indirect(n2_list[:]), neg_n1[:], ALU.add)
+            neg_diff.append(diff)
 
-        z2_grouped = sb("z2g", [P, H, PACK], BF16)
         z2_codes = sb("z2_codes", [P, H], U32)
         z2_scales = sb("z2_scales", [P, H], U8)
 
-        def z2_finish():
-            nc.vector.tensor_copy(
-                out=z2_grouped[:].bitcast(F32), in_=z2_pairs[:].bitcast(F32).rearrange("p u c o -> p c (u o)")
-            )
-            quantise(z2_codes[:], z2_scales[:], z2_grouped[:].rearrange("p c t -> p (c t)"))
-
-        evac_b(0)
-        z2_plane(0)
-        evac_b(1)
-        z2_plane(1)
-        difference(0)
-        difference(1)
-        evac_b(2)
-        evac_b(3)
+        for t in (0, 1):
+            copy_b_out(t)
+            scale_z2(t)
+        for t in (0, 1):
+            difference(t)
+        for t in (2, 3):
+            b_psum.append(b_product(t))
+            copy_b_out(t)
         difference(2)
-        z2_plane(2)
-        z2_plane(3)
-        difference(3)
-        z2_finish()
+        for t in (2, 3):
+            scale_z2(t)
+        z2_grouped = [sb("z2_grouped%d" % h, [P, width(cols), PACK], BF16) for h, cols in enumerate(HALVES)]
+        for h, cols in enumerate(HALVES):
+            nc.vector.tensor_copy(
+                out=z2_grouped[h][:].bitcast(F32), in_=z2_pairs[:, :, cols, :].bitcast(F32).rearrange("p u c o -> p c (u o)")
+            )
+        for h, cols in enumerate(HALVES):
+            quantise(z2_codes[:, cols], z2_scales[:, cols], z2_grouped[h][:].rearrange("p c t -> p (c t)"))
+        difference(LAST)
 
         z_codes = sb("z_codes", [P, H], U32)
         z_scales = sb("z_scales", [P, H], U8)
-        cv_ps = []
+        cv_psum = []
+        cv_parts = (((HALVES[0], 2), (HALVES[1], 3)), ((ALL, 0),), ((ALL, 1),), ((ALL, 2),))
 
-        def z_pair(u, th_tag):
-            rs = slice(PAIR * u, PAIR * (u + 1))
-            th = sb("th%d" % u, [P, PACK, PAIR, P], F32, tag=th_tag)
-            planes = sb("zp%d" % u, [P, PACK, PAIR, P], BF16, tag="zp")
+        def z_and_cv(pair):
+            rows = range(PAIR * pair, PAIR * (pair + 1))
+            features = slice(rows.start, rows.stop)
+            tanh_diff = sb("tanh_diff%d" % pair, [P, PACK, PAIR, P], F32, reuse="neg_n1_%d" % (PAIR + pair))
+            z_by_tile = sb("z_by_tile%d" % pair, [P, PACK, PAIR, P], BF16, reuse="z2_grouped1")
             for t in range(PACK):
                 nc.scalar.activation(
-                    th[:, t].rearrange("p r m -> p m r"), diff[t][:].rearrange("p (m r) -> p m r", r=PACK)[:, :, rs], ACT.Tanh, scale=-1.0
+                    tanh_diff[:, t].rearrange("p r m -> p m r"),
+                    neg_diff[t][:].rearrange("p (m r) -> p m r", r=PACK)[:, :, features],
+                    ACT.Tanh,
+                    scale=-1.0,
                 )
                 nc.vector.scalar_tensor_tensor(
-                    out=planes[:, t],
-                    in0=a_ps[t][:].rearrange("p (m r) -> p r m", r=PACK)[:, rs, :],
-                    scalar=gt_t[:, t : t + 1],
-                    in1=th[:, t],
+                    out=z_by_tile[:, t],
+                    in0=a_psum[t][:].rearrange("p (m r) -> p r m", r=PACK)[:, features, :],
+                    scalar=gt_by_tile[:, t : t + 1],
+                    in1=tanh_diff[:, t],
                     op0=ALU.mult,
                     op1=ALU.mult,
                 )
-            grouped = sb("zg%d" % u, [P, PAIR * P, PACK], BF16)
-            nc.vector.tensor_copy(
-                out=grouped[:].rearrange("p (c i) t -> p c t i", i=4),
-                in_=planes[:].rearrange("p t r (c i) -> p (r c) t i", i=4),
-            )
-            cols = slice(u * HALF, (u + 1) * HALF)
-            quantise(z_codes[:, cols], z_scales[:, cols], grouped[:].rearrange("p c t -> p (c t)"))
-            for r in range(PAIR * u, PAIR * (u + 1)):
-                parts = HALVES if r == 0 else WHOLE
-                cv_ps.append([
-                    (cols, product("cv_ps%d_%d" % (r, i), CV_BANKS[r][i], z_codes, z_scales, r, z2_codes, z2_scales, cols))
-                    for i, cols in enumerate(parts)
+            z_grouped = sb("z_grouped%d" % pair, [P, PAIR, P, PACK], BF16)
+            for k in range(PAIR):
+                nc.vector.tensor_copy(
+                    out=z_grouped[:, k].rearrange("p (c i) t -> p c t i", i=4),
+                    in_=z_by_tile[:, :, k, :].rearrange("p t (c i) -> p c t i", i=4),
+                )
+            for k, r in enumerate(rows):
+                cols = slice(r * P, (r + 1) * P)
+                quantise(z_codes[:, cols], z_scales[:, cols], z_grouped[:, k].rearrange("p c t -> p (c t)"))
+            for r in rows:
+                cv_psum.append([
+                    (cols, product("cv_psum%d_%d" % (r, bank), bank, z_codes, z_scales, r, z2_codes, z2_scales, cols))
+                    for cols, bank in cv_parts[r]
                 ])
 
         out_rows = out_0.rearrange("(p r) c -> p r c", r=PACK)
-        cv, pa, old, tp, ra = {}, {}, {}, {}, {}
+        cv, pa, old, tanh_pa, ra = {}, {}, {}, {}, {}
 
-        def evac(r, on_scalar=False, tag=None):
-            cv[r] = sb("cv%d" % r, [P, H], F32, tag=tag)
-            for cols, acc in cv_ps[r]:
-                if on_scalar:
+        def copy_cv_out(r):
+            cv[r] = sb("cv%d" % r, [P, H], F32)
+            for cols, acc in cv_psum[r]:
+                if r < PAIR:
                     nc.scalar.activation(cv[r][:, cols], acc[:], ACT.Copy, scale=0.0625)
                 else:
                     nc.vector.tensor_scalar(out=cv[r][:, cols], in0=acc[:], scalar1=0.0625, scalar2=None, op0=ALU.mult)
 
-        def g_pa(r, tag=None):
-            pa[r] = sb("pa%d" % r, [P, W], F32, tag=tag)
-            nc.vector.tensor_copy(pa[r][:], cv[r][:].indirect(n4_t[:]))
+        def gather_pa(r):
+            pa[r] = sb("pa%d" % r, [P, W], F32)
+            nc.vector.tensor_copy(pa[r][:], cv[r][:].indirect(n4_list[:]))
 
-        def g_old(r, tag=None):
-            if r not in old:
-                old[r] = sb("old%d" % r, [P, W], F32, tag=tag)[:]
-            nc.scalar.activation(old[r], cv[r][:].indirect(n3_t[:]), ACT.Copy)
+        def gather_old(r, out):
+            old[r] = out
+            nc.scalar.activation(old[r], cv[r][:].indirect(n3_list[:]), ACT.Copy)
 
-        def t_pa(r, tag=None):
-            tp[r] = sb("tp%d" % r, [P, W], F32, tag=tag)
-            nc.scalar.activation(tp[r][:], pa[r][:], ACT.Tanh)
+        def tanh_of_pa(r, reuse=None):
+            tanh_pa[r] = sb("tanh_pa%d" % r, [P, W], F32, reuse)
+            nc.scalar.activation(tanh_pa[r][:], pa[r][:], ACT.Tanh)
 
-        def hold(r, tag):
-            held = sb("held%d" % r, [P, 2, W], F32, tag=tag)
-            old[r] = held[:, 0, :]
-            ra[r - 1] = held[:, 1, :]
+        def subtract(r, out):
+            ra[r] = out
+            nc.vector.tensor_tensor(ra[r], old[r], tanh_pa[r][:], ALU.subtract)
 
-        def sub(r, tag=None):
-            if r not in ra:
-                ra[r] = sb("ra%d" % r, [P, W], F32, tag=tag)[:]
-            nc.vector.tensor_tensor(ra[r], old[r], tp[r][:], ALU.subtract)
-
-        def put(r):
-            nc.scalar.activation(cv[r][:].indirect(n3_t[:]), ra[r], ACT.Copy)
+        def scatter_and_store(r):
+            nc.scalar.activation(cv[r][:].indirect(n3_list[:]), ra[r], ACT.Copy)
             nc.sync.dma_start(out=out_rows[:, r, :], in_=cv[r][:])
 
-        z_pair(0, "g1_2")
-        evac(0, True)
-        g_pa(0)
-        g_old(0)
-        t_pa(0)
-        z_pair(1, "g1_3")
-        sub(0)
-        evac(1, tag="zp")
-        g_pa(1)
-        g_old(1)
-        put(0)
-        t_pa(1)
-        evac(2)
-        g_pa(2)
-        t_pa(2)
-        hold(2, "pa2")
-        g_old(2)
-        sub(1)
-        put(1)
-        evac(3)
-        g_pa(3)
-        t_pa(3, "tp1")
-        hold(3, "pa3")
-        g_old(3)
-        sub(2)
-        put(2)
-        sub(3)
-        put(3)
+        def entries(name, reuse=None):
+            return sb(name, [P, W], F32, reuse)[:]
 
-        last = PACK - 1
-        og = sb("og", [P, H, PACK], BF16, tag="old1")
-        for r in range(last):
-            nc.vector.tensor_copy(out=og[:, :, r], in_=cv[r][:])
-        o_codes = sb("o_codes", [P, H], U32)
-        o_scales = sb("o_scales", [P, H], U8)
+        z_and_cv(0)
+        copy_cv_out(0)
+        gather_pa(0)
+        gather_old(0, entries("old0"))
+        copy_cv_out(1)
+        tanh_of_pa(0)
+        z_and_cv(1)
+        subtract(0, entries("ra0"))
+        gather_old(1, entries("old1", reuse="pa0"))
+        gather_pa(1)
+        scatter_and_store(0)
+        tanh_of_pa(1)
+
+        copy_cv_out(2)
+        gather_old(2, entries("old2"))
+        gather_pa(2)
+        subtract(1, entries("ra1"))
+        scatter_and_store(1)
+        tanh_of_pa(2)
+
+        copy_cv_out(LAST)
+        gather_pa(LAST)
+        tanh_of_pa(LAST, reuse="tanh_pa1")
+        after_tanh = sb("after_tanh", [P, 2, W], F32, reuse="pa%d" % LAST)
+        gather_old(LAST, after_tanh[:, 0, :])
+        subtract(2, after_tanh[:, 1, :])
+        scatter_and_store(2)
+        subtract(LAST, entries("ra%d" % LAST))
+        scatter_and_store(LAST)
+
+        out_grouped = sb("out_grouped", [P, H, PACK], BF16, reuse="tanh_pa0")
+        for r in range(LAST):
+            nc.vector.tensor_copy(out=out_grouped[:, :, r], in_=cv[r][:])
+        out_codes = sb("out_codes", [P, H], U32)
+        out_scales = sb("out_scales", [P, H], U8)
         out_words = out_1[0].rearrange("p c r -> p (c r)").bitcast(I32)
-        for h in range(2):
-            cols = slice(h * HALF, (h + 1) * HALF)
-            nc.vector.tensor_copy(out=og[:, cols, last], in_=cv[last][:, cols])
-        for h in range(2):
-            cols = slice(h * HALF, (h + 1) * HALF)
-            quantise(o_codes[:, cols], o_scales[:, cols], og[:, cols, :].rearrange("p c r -> p (c r)"))
-            nc.sync.dma_start(out=out_words[:, cols], in_=o_codes[:, cols].bitcast(I32))
-        for q in range(4):
-            eng = nc.sync if q % 2 else nc.scalar
-            eng.dma_start(out=out_2[0, 4 * q : 4 * q + 4, :].bitcast(I32), in_=o_scales[32 * q : 32 * q + 4, :].bitcast(I32))
+        for cols in HALVES:
+            nc.vector.tensor_copy(out=out_grouped[:, cols, LAST], in_=cv[LAST][:, cols])
+        for cols in HALVES:
+            quantise(out_codes[:, cols], out_scales[:, cols], out_grouped[:, cols, :].rearrange("p c r -> p (c r)"))
+            nc.sync.dma_start(out=out_words[:, cols], in_=out_codes[:, cols].bitcast(I32))
+        for q in range(QUADRANTS):
+            queue = nc.sync if q % 2 else nc.scalar
+            queue.dma_start(
+                out=out_2[0, 4 * q : 4 * q + 4, :].bitcast(I32), in_=out_scales[32 * q : 32 * q + 4, :].bitcast(I32)
+            )

from contextlib import ExitStack

import concourse.mybir as mybir
from concourse.masks import make_identity

T, S, H, W = 2048, 512, 512, 384
FLOPS = 3 * 2 * 512 * 512 * 512

F32 = mybir.dt.float32
BF16 = mybir.dt.bfloat16
I32 = mybir.dt.int32
U32 = mybir.dt.uint32
U16 = mybir.dt.uint16
U8 = mybir.dt.uint8
FP8X4 = mybir.dt.float8_e4m3fn_x4
ACT = mybir.ActivationFunctionType
ALU = mybir.AluOpType

P = 128
PACK = 4
RUN = 8
QUADRANTS = 4
SPARE = 8
PAIR = 2
LAST = PACK - 1
ALL = slice(0, H)
HALVES = (slice(0, H // 2), slice(H // 2, H))
WA_SCALAR, WA_VECTOR = slice(0, 128), slice(128, H)
N2_ON_SCALAR = (2, 3)
B_OUT_ON_VECTOR = 1


def tile_picked_momtjointbktanh_none_po_kernel(
    tc, x_words, x_scales, wa, wb, gt, gi, offs, two, n1, n2, n3, n4, out_0, out_1, out_2
):
    nc = tc.nc
    with ExitStack() as ctx:
        keep = ctx.enter_context(tc.tile_pool(name="keep", bufs=1))
        psum = ctx.enter_context(tc.psum_pool(name="psum", bufs=1))

        def sb(name, shape, dtype, reuse=None):
            return keep.tile(shape, dtype, name=name, tag=reuse or name, align_bytes=64)

        def width(cols):
            return cols.stop - cols.start

        def load_list(name, src):
            offsets = keep.tile(list(src.shape), U16, name=name)
            nc.sync.dma_start(offsets[:], src)
            return offsets

        def load_weight(name, w, cols):
            raw = sb(name, [P, PACK, width(cols)], F32)
            nc.sync.dma_start(out=raw[:], in_=w.rearrange("(p j) n -> p j n", j=PACK)[:, :, cols])
            return raw

        x_scale_table = sb("x_scale_table", [P, T], U8)
        nc.gpsimd.memset(x_scale_table[:].bitcast(I32), 0)
        gain_rows = sb("gain_rows", [P, P], F32)
        nc.gpsimd.memset(gain_rows[:], 0.0)
        identity = sb("identity", [P, P], F32)
        make_identity(nc, identity[:])

        two_list = load_list("two_list", two)
        offs_list = load_list("offs_list", offs)
        for q in range(QUADRANTS):
            queue = nc.sync if q % 2 else nc.scalar
            queue.dma_start(
                out=x_scale_table[32 * q : 32 * q + 4, :].bitcast(I32), in_=x_scales[0, 4 * q : 4 * q + 4, :].bitcast(I32)
            )
        for first_row, gain in ((0, gi), (PACK, gt)):
            nc.scalar.dma_start(
                out=gain_rows[first_row : first_row + PACK, :].rearrange("t (g e) -> t g e", e=RUN),
                in_=gain.rearrange("(g t e) o -> t g (e o)", t=PACK, e=RUN),
            )
        wb_raw = [load_weight("wb_raw%d" % h, wb, cols) for h, cols in enumerate(HALVES)]
        x_word_table = sb("x_word_table", [P, T], I32)
        nc.sync.dma_start(out=x_word_table[:], in_=x_words[0].rearrange("p c j -> p (c j)").bitcast(I32))
        wa_raw_scalar = load_weight("wa_raw_scalar", wa, WA_SCALAR)
        n1_list = load_list("n1_list", n1)
        n2_list = load_list("n2_list", n2)
        wa_raw_vector = load_weight("wa_raw_vector", wa, WA_VECTOR)
        n3_list = load_list("n3_list", n3)
        n4_list = load_list("n4_list", n4)

        b_tiles = []
        for t in range(PACK):
            b_tile = sb("b%d" % t, [P, H + SPARE], F32)
            nc.gpsimd.memset(b_tile[:, H:], 0.0)
            b_tiles.append(b_tile)

        def gather_scales(name, offsets):
            picked = sb(name + "_picked", [P, S], U8, reuse="picked_scales")
            nc.vector.tensor_copy(picked[:], x_scale_table[:].indirect(offsets[:]))
            dealt = sb(name, [P, S], U8)
            nc.vector.tensor_copy(
                out=dealt[:].bitcast(I32).rearrange("p (t g w) -> p t g w", t=PACK, w=RUN // 4),
                in_=picked[:].bitcast(I32).rearrange("p (g t w) -> p t g w", t=PACK, w=RUN // 4),
            )
            return dealt

        def gather_words(name, offsets):
            dealt = sb(name, [P, S], U32)
            nc.vector.tensor_copy(
                dealt[:].rearrange("p (t g e) -> p g t e", t=PACK, e=RUN), x_word_table[:].bitcast(U32).indirect(offsets[:])
            )
            return dealt

        def quantise(codes, scales, grouped):
            nc.vector.quantize_mx(out=codes.bitcast(FP8X4), scales=scales, in_=grouped)

        def quantise_weight(name, raw, cols, codes, scales, copy):
            grouped = sb(name, [P, width(cols), PACK], BF16)
            copy(out=grouped[:].rearrange("p (c i) j -> p c j i", i=4), in_=raw[:].rearrange("p j (c i) -> p c j i", i=4))
            quantise(codes[:, cols], scales[:, cols], grouped[:].rearrange("p c j -> p (c j)"))

        def product(name, bank, l_codes, l_scales, tile, r_codes, r_scales, moving):
            acc = psum.tile([P, width(moving)], F32, name=name, tag="bank%d" % bank)
            stationary = slice(tile * P, (tile + 1) * P)
            nc.tensor.matmul_mx(
                out=acc[:],
                lhsT=l_codes[:, stationary].bitcast(FP8X4),
                lhsT_scale=l_scales[:, stationary],
                rhs=r_codes[:, moving].bitcast(FP8X4),
                rhs_scale=r_scales[:, moving],
                start=True,
                stop=True,
            )
            return acc

        gain_psum = psum.tile([P, P], F32, name="gain_psum", tag="bank2")
        nc.tensor.transpose(gain_psum[:], gain_rows[:], identity[:])

        xb_scales = gather_scales("xb_scales", two_list)
        xa_scales = gather_scales("xa_scales", offs_list)
        xb_codes = gather_words("xb_codes", two_list)
        wb_codes = sb("wb_codes", [P, H], U32)
        wb_scales = sb("wb_scales", [P, H], U8)
        for h, cols in enumerate(HALVES):
            quantise_weight("wb_grouped%d" % h, wb_raw[h], cols, wb_codes, wb_scales, nc.scalar.copy)

        def b_product(t):
            return product("b_psum%d" % t, t % 2, xb_codes, xb_scales, t, wb_codes, wb_scales, ALL)

        b_psum = [b_product(0), b_product(1)]

        xa_codes = gather_words("xa_codes", offs_list)
        wa_codes = sb("wa_codes", [P, H], U32)
        wa_scales = sb("wa_scales", [P, H], U8)
        quantise_weight("wa_grouped_scalar", wa_raw_scalar, WA_SCALAR, wa_codes, wa_scales, nc.scalar.copy)
        gains = sb("gains", [P, 2 * PACK], F32, reuse="wa_raw_scalar")
        nc.scalar.copy(out=gains[:], in_=gain_psum[:, : 2 * PACK])
        gi_by_tile, gt_by_tile = gains[:, :PACK], gains[:, PACK:]
        quantise_weight("wa_grouped_vector", wa_raw_vector, WA_VECTOR, wa_codes, wa_scales, nc.vector.tensor_copy)
        a_psum = [product("a_psum%d" % t, PACK + t, xa_codes, xa_scales, t, wa_codes, wa_scales, ALL) for t in range(PACK)]

        z2_pairs = sb("z2_pairs", [P, 2, H, 2], BF16)
        neg_diff = []

        def copy_b_out(t):
            copy = nc.vector.tensor_copy if t == B_OUT_ON_VECTOR else nc.scalar.copy
            copy(out=b_tiles[t][:, :H], in_=b_psum[t][:])

        def scale_z2(t):
            nc.vector.tensor_scalar(
                out=z2_pairs[:, t // 2, :, t % 2], in0=b_tiles[t][:, :H], scalar1=gi_by_tile[:, t : t + 1], scalar2=None, op0=ALU.mult
            )

        def difference(t):
            neg_n1 = sb("neg_n1_%d" % t, [P, H], F32)
            nc.scalar.activation(neg_n1[:], b_tiles[t][:].indirect(n1_list[:]), ACT.Copy, scale=-1.0)
            diff = sb("neg_diff%d" % t, [P, H], F32, reuse="z2_grouped0" if t == LAST else None)
            if t in N2_ON_SCALAR:
                at_n2 = sb("at_n2_%d" % t, [P, H], F32)
                nc.scalar.activation(at_n2[:], b_tiles[t][:].indirect(n2_list[:]), ACT.Copy)
                nc.vector.tensor_tensor(diff[:], at_n2[:], neg_n1[:], ALU.add)
            else:
                nc.vector.tensor_tensor(diff[:], b_tiles[t][:].indirect(n2_list[:]), neg_n1[:], ALU.add)
            neg_diff.append(diff)

        z2_codes = sb("z2_codes", [P, H], U32)
        z2_scales = sb("z2_scales", [P, H], U8)

        for t in (0, 1):
            copy_b_out(t)
            scale_z2(t)
        for t in (0, 1):
            difference(t)
        for t in (2, 3):
            b_psum.append(b_product(t))
            copy_b_out(t)
        difference(2)
        for t in (2, 3):
            scale_z2(t)
        z2_grouped = [sb("z2_grouped%d" % h, [P, width(cols), PACK], BF16) for h, cols in enumerate(HALVES)]
        for h, cols in enumerate(HALVES):
            nc.vector.tensor_copy(
                out=z2_grouped[h][:].bitcast(F32), in_=z2_pairs[:, :, cols, :].bitcast(F32).rearrange("p u c o -> p c (u o)")
            )
        for h, cols in enumerate(HALVES):
            quantise(z2_codes[:, cols], z2_scales[:, cols], z2_grouped[h][:].rearrange("p c t -> p (c t)"))
        difference(LAST)

        z_codes = sb("z_codes", [P, H], U32)
        z_scales = sb("z_scales", [P, H], U8)
        cv_psum = []
        cv_parts = (((HALVES[0], 2), (HALVES[1], 3)), ((ALL, 0),), ((ALL, 1),), ((ALL, 2),))

        def z_and_cv(pair):
            rows = range(PAIR * pair, PAIR * (pair + 1))
            features = slice(rows.start, rows.stop)
            tanh_diff = sb("tanh_diff%d" % pair, [P, PACK, PAIR, P], F32, reuse="neg_n1_%d" % (PAIR + pair))
            z_by_tile = sb("z_by_tile%d" % pair, [P, PACK, PAIR, P], BF16, reuse="z2_grouped1")
            for t in range(PACK):
                nc.scalar.activation(
                    tanh_diff[:, t].rearrange("p r m -> p m r"),
                    neg_diff[t][:].rearrange("p (m r) -> p m r", r=PACK)[:, :, features],
                    ACT.Tanh,
                    scale=-1.0,
                )
                nc.vector.scalar_tensor_tensor(
                    out=z_by_tile[:, t],
                    in0=a_psum[t][:].rearrange("p (m r) -> p r m", r=PACK)[:, features, :],
                    scalar=gt_by_tile[:, t : t + 1],
                    in1=tanh_diff[:, t],
                    op0=ALU.mult,
                    op1=ALU.mult,
                )
            z_grouped = sb("z_grouped%d" % pair, [P, PAIR, P, PACK], BF16)
            for k in range(PAIR):
                nc.vector.tensor_copy(
                    out=z_grouped[:, k].rearrange("p (c i) t -> p c t i", i=4),
                    in_=z_by_tile[:, :, k, :].rearrange("p t (c i) -> p c t i", i=4),
                )
            for k, r in enumerate(rows):
                cols = slice(r * P, (r + 1) * P)
                quantise(z_codes[:, cols], z_scales[:, cols], z_grouped[:, k].rearrange("p c t -> p (c t)"))
            for r in rows:
                cv_psum.append([
                    (cols, product("cv_psum%d_%d" % (r, bank), bank, z_codes, z_scales, r, z2_codes, z2_scales, cols))
                    for cols, bank in cv_parts[r]
                ])

        out_rows = out_0.rearrange("(p r) c -> p r c", r=PACK)
        cv, pa, old, tanh_pa, ra = {}, {}, {}, {}, {}

        def copy_cv_out(r):
            cv[r] = sb("cv%d" % r, [P, H], F32)
            for cols, acc in cv_psum[r]:
                if r < PAIR:
                    nc.scalar.activation(cv[r][:, cols], acc[:], ACT.Copy, scale=0.0625)
                else:
                    nc.vector.tensor_scalar(out=cv[r][:, cols], in0=acc[:], scalar1=0.0625, scalar2=None, op0=ALU.mult)

        def gather_pa(r):
            pa[r] = sb("pa%d" % r, [P, W], F32)
            nc.vector.tensor_copy(pa[r][:], cv[r][:].indirect(n4_list[:]))

        def gather_old(r, out):
            old[r] = out
            nc.scalar.activation(old[r], cv[r][:].indirect(n3_list[:]), ACT.Copy)

        def tanh_of_pa(r, reuse=None):
            tanh_pa[r] = sb("tanh_pa%d" % r, [P, W], F32, reuse)
            nc.scalar.activation(tanh_pa[r][:], pa[r][:], ACT.Tanh)

        def subtract(r, out):
            ra[r] = out
            nc.vector.tensor_tensor(ra[r], old[r], tanh_pa[r][:], ALU.subtract)

        def scatter_and_store(r):
            nc.scalar.activation(cv[r][:].indirect(n3_list[:]), ra[r], ACT.Copy)
            nc.sync.dma_start(out=out_rows[:, r, :], in_=cv[r][:])

        def entries(name, reuse=None):
            return sb(name, [P, W], F32, reuse)[:]

        z_and_cv(0)
        copy_cv_out(0)
        gather_pa(0)
        gather_old(0, entries("old0"))
        copy_cv_out(1)
        tanh_of_pa(0)
        z_and_cv(1)
        subtract(0, entries("ra0"))
        gather_old(1, entries("old1", reuse="pa0"))
        gather_pa(1)
        scatter_and_store(0)
        tanh_of_pa(1)

        copy_cv_out(2)
        gather_old(2, entries("old2"))
        gather_pa(2)
        subtract(1, entries("ra1"))
        scatter_and_store(1)
        tanh_of_pa(2)

        copy_cv_out(LAST)
        gather_pa(LAST)
        tanh_of_pa(LAST, reuse="tanh_pa1")
        after_tanh = sb("after_tanh", [P, 2, W], F32, reuse="pa%d" % LAST)
        gather_old(LAST, after_tanh[:, 0, :])
        subtract(2, after_tanh[:, 1, :])
        scatter_and_store(2)
        subtract(LAST, entries("ra%d" % LAST))
        scatter_and_store(LAST)

        out_grouped = sb("out_grouped", [P, H, PACK], BF16, reuse="tanh_pa0")
        for r in range(LAST):
            nc.vector.tensor_copy(out=out_grouped[:, :, r], in_=cv[r][:])
        out_codes = sb("out_codes", [P, H], U32)
        out_scales = sb("out_scales", [P, H], U8)
        out_words = out_1[0].rearrange("p c r -> p (c r)").bitcast(I32)
        for cols in HALVES:
            nc.vector.tensor_copy(out=out_grouped[:, cols, LAST], in_=cv[LAST][:, cols])
        for cols in HALVES:
            quantise(out_codes[:, cols], out_scales[:, cols], out_grouped[:, cols, :].rearrange("p c r -> p (c r)"))
            nc.sync.dma_start(out=out_words[:, cols], in_=out_codes[:, cols].bitcast(I32))
        for q in range(QUADRANTS):
            queue = nc.sync if q % 2 else nc.scalar
            queue.dma_start(
                out=out_2[0, 4 * q : 4 * q + 4, :].bitcast(I32), in_=out_scales[32 * q : 32 * q + 4, :].bitcast(I32)
            )
